import numpy as np
import ml_dtypes


def mxq(x, axis, fmt="e4m3"):
    dtype, down = {"e4m3": (ml_dtypes.float8_e4m3fn, 7), "e5m2": (ml_dtypes.float8_e5m2, 14)}[fmt]
    v = np.moveaxis(np.asarray(x, np.float32).astype(ml_dtypes.bfloat16).astype(np.float64), axis, -1)
    blocks = v.reshape(v.shape[:-1] + (-1, 32))
    amax = np.abs(blocks).max(-1, keepdims=True)
    byte = np.maximum(np.where(amax > 0, np.frexp(amax)[1] - 1 + 127, 0) - down, 1)
    scale = np.exp2(byte - 127.0)
    codes = (blocks / scale).astype(np.float32).astype(dtype).astype(np.float64)
    return np.moveaxis((codes * scale).reshape(v.shape), -1, axis)


WIDE = False


def mx_kscale(k):
    if not WIDE:
        return np.ones(k)
    levels = np.array([10, -10, 5, -5, 0])
    if k % 512:
        return np.exp2(np.random.permutation(np.resize(levels, k // 32))).repeat(32)
    a = np.empty((k // 512, 16))
    for p in range(k // 512):
        a[p, :8] = np.random.permutation(np.resize(levels, 8))
        for g in range(8):
            far = levels[np.abs(levels - a[p, g]) >= 10]
            a[p, g + 8] = far[np.random.randint(len(far))]
    return np.exp2(a.ravel()).repeat(32)


def f64(x):
    return np.asarray(x).astype(np.float64)


def striped(idx):
    return np.tile(idx.reshape(-1, 16).T, (8, 1)).astype(np.uint16)


def unstriped(offs):
    return offs[:16].T.reshape(-1).astype(np.int64)


def striped8(idx):
    return np.concatenate([x.reshape(-1, 16).T for x in idx]).astype(np.uint16)


def runs(offs, k):
    lists = np.stack([offs[16 * r : 16 * r + 16].T.reshape(-1) for r in range(8)]).astype(np.int64)
    return lists[np.arange(k) % 512 // 64]


def pack_weight(w):
    k, n = w.shape
    w = f64(np.asarray(w, np.float32).astype(ml_dtypes.bfloat16)).reshape(k // 32, 32, n)
    amax = np.abs(w).max(1)
    byte = np.clip(np.where(amax > 0, np.frexp(amax)[1] - 1 + 127 - 7, 1), 1, 254)
    scaled = (w * np.exp2(127.0 - byte)[:, None, :]).reshape(k, n).astype(np.float32)
    words = np.ascontiguousarray(scaled.reshape(k // 512, 128, 4, n).transpose(0, 1, 3, 2)).astype(ml_dtypes.float8_e4m3fn).view(np.uint8)
    return words, np.ascontiguousarray(byte.astype(np.uint8).reshape(k // 512, 16, n))


def unpack_weight(words, scales):
    g, p, n, _ = words.shape
    vals = np.ascontiguousarray(words).view(ml_dtypes.float8_e4m3fn).astype(np.float64) * np.repeat(np.exp2(scales.astype(np.float64) - 127.0), 8, axis=1)[..., None]
    return vals.transpose(0, 1, 3, 2).reshape(g * 512, n)


E2M1 = np.array([0.0, 0.5, 1.0, 1.5, 2.0, 3.0, 4.0, 6.0, -0.0, -0.5, -1.0, -1.5, -2.0, -3.0, -4.0, -6.0])


def pack_fp4(w):
    k, n = w.shape
    w = f64(np.asarray(w, np.float32).astype(ml_dtypes.bfloat16)).reshape(k // 32, 32, n)
    amax = np.abs(w).max(1)
    mant, ex = np.frexp(amax / 6.0)
    byte = np.clip(np.where(amax > 0, np.where(mant > 0.5, ex, ex - 1) + 127, 1), 1, 254)
    scaled = (w * np.exp2(127.0 - byte)[:, None, :]).reshape(k, n).astype(np.float32)
    c = np.ascontiguousarray(scaled.reshape(k // 512, 128, 4, n).transpose(0, 1, 3, 2)).astype(ml_dtypes.float4_e2m1fn).view(np.uint8) & 0xF
    words = (c[..., 0::2] | (c[..., 1::2] << 4)).reshape(k // 512, 128, 2 * n)
    return np.ascontiguousarray(words), np.ascontiguousarray(byte.astype(np.uint8).reshape(k // 512, 16, n))


def unpack_fp4(words, scales):
    g, _, n = scales.shape
    words = np.ascontiguousarray(words).reshape(g, 128, n, 2)
    nib = np.empty((g, 128, n, 4), np.uint8)
    nib[..., 0::2] = words & 0xF
    nib[..., 1::2] = words >> 4
    vals = E2M1[nib] * np.repeat(np.exp2(scales.astype(np.float64) - 127.0), 8, axis=1)[..., None]
    return vals.transpose(0, 1, 3, 2).reshape(g * 512, n)


def planes(y):
    n, m = y.shape
    v = y.astype(np.float32).astype(ml_dtypes.bfloat16).astype(np.float64).reshape(n // 32, 32, m)
    top = np.abs(v).max(1)
    byte = np.clip(np.where(top > 0, np.frexp(top)[1] - 1 + 127 - 7, 1), 1, 254)
    codes = (v * np.exp2(127.0 - byte)[:, None, :]).reshape(n, m).astype(np.float32).astype(ml_dtypes.float8_e4m3fn).view(np.uint8)
    words = codes.reshape(n // 512, 128, 4, m).transpose(0, 1, 3, 2)
    return np.ascontiguousarray(words), np.ascontiguousarray(byte.astype(np.uint8).reshape(n // 512, 16, m))


K, T, S, N, H = 512, 2048, 512, 512, 512


def setup_inputs():
    n = np.random.standard_normal
    s = mx_kscale(K)[:, None]
    u = mx_kscale(H)
    packed_xT = pack_weight(n((K, T)) * s)
    packed_w1 = pack_fp4(n((K, H)) / np.sqrt(K) / s)
    packed_w2 = pack_fp4(n((H, N)) / np.sqrt(2 * H) / u[:, None])
    packed_w3 = pack_fp4(n((K, N)) / np.sqrt(2 * K) / s)
    return {
        "x_words": packed_xT[0],
        "x_scales": packed_xT[1],
        "w1_words": packed_w1[0],
        "w1_scales": packed_w1[1],
        "gn": (np.random.uniform(0.5, 1.5, (H, 1)) * u[:, None]).astype(np.float32),
        "w2_words": packed_w2[0],
        "w2_scales": packed_w2[1],
        "w3_words": packed_w3[0],
        "w3_scales": packed_w3[1],
        "offs": striped8(np.random.randint(0, T, (8, S))),
        "n1": striped8(np.stack([np.random.permutation(S) for _ in range(8)])),
        "n2": striped8(np.stack([np.random.permutation(S) for _ in range(8)])),
        "two": striped(np.random.permutation(T)[:S]),
        "n3": striped(np.random.permutation(S)),
        "n4": striped(np.random.permutation(S)),
    }


def reference(x_words, x_scales, w1_words, w1_scales, gn, w2_words, w2_scales, w3_words, w3_scales, offs, n1, n2, two, n3, n4):
    xq = unpack_weight(x_words, x_scales)[np.arange(K)[:, None], runs(offs, K)]
    y = unpack_fp4(w1_words, w1_scales).T @ xq
    z = f64(gn) * (0.75 * (y[np.arange(H)[:, None], runs(n1, H)] + y[np.arange(H)[:, None], runs(n2, H)]) - y)
    x_two = unpack_weight(x_words, x_scales)[:, unstriped(two)]
    h = unpack_fp4(w2_words, w2_scales).T @ mxq(z, 0, "e4m3") + unpack_fp4(w3_words, w3_scales).T @ x_two
    st = h - h[:, unstriped(n3)]
    out_0 = st / (np.abs(st[:, unstriped(n4)]) + 0.5)
    return (out_0,) + planes(out_0)

@@ -1,0 +1,228 @@
+from contextlib import ExitStack
+
+import concourse.mybir as mybir
+
+F32 = mybir.dt.float32
+BF16 = mybir.dt.bfloat16
+I32 = mybir.dt.int32
+U32 = mybir.dt.uint32
+U16 = mybir.dt.uint16
+U8 = mybir.dt.uint8
+FP8X4 = mybir.dt.float8_e4m3fn_x4
+FP4X4 = mybir.dt.float4_e2m1fn_x4
+ALU = mybir.AluOpType
+ACT = mybir.ActivationFunctionType
+
+P = 128
+K, T, S, N, H = 512, 2048, 512, 512, 512
+PACK = 4
+HALF = S // 2
+PIECES = ((0, 256), (256, 128), (384, 128))
+OUT_PIECES = ((0, 128), (128, 128), (256, 128), (384, 128))
+FLOPS = 3 * 2 * K * H * S
+
+
+def tile_picked_hmixlaphopn_none_po_kernel(
+    tc, x_words, x_scales, w1_words, w1_scales, gn, w2_words, w2_scales, w3_words, w3_scales,
+    offs, n1, n2, two, n3, n4, out_0, out_1, out_2,
+):
+    nc = tc.nc
+
+    with ExitStack() as ctx:
+        lists = ctx.enter_context(tc.tile_pool(name="lists", bufs=1))
+        keep = ctx.enter_context(tc.tile_pool(name="keep", bufs=1))
+        psum = ctx.enter_context(tc.psum_pool(name="psum", bufs=1))
+
+        def load_list(name, src):
+            tile = lists.tile([P, S // 16], U16, name=name)
+            nc.sync.dma_start(tile[:], src)
+            return tile
+
+        def entries(tile, first, count):
+            return tile[:, first // 16 : (first + count) // 16]
+
+        def load_scales(queue, name, src, width, tag):
+            tile = keep.tile([P, width], U8, name=name, tag=tag, align_bytes=64)
+            rows = src[0].bitcast(I32).unsqueeze(1).to_broadcast([16, 8, width // 4])
+            queue.dma_start(tile[:].bitcast(I32), rows)
+            return tile
+
+        def load_fp4(queue, name, src, tag):
+            tile = keep.tile([P, 2 * H], U8, name=name, tag=tag, align_bytes=64)
+            queue.dma_start(tile[:].bitcast(I32), src[0].bitcast(I32))
+            return tile
+
+        def deal_words(name, raw):
+            tile = keep.tile([P, 2 * H], U8, name=name, tag=name, align_bytes=64)
+            nc.vector.tensor_copy(
+                tile[:].rearrange("p (t m b) -> p t m b", t=PACK, b=2),
+                raw[:].rearrange("p (m t b) -> p t m b", t=PACK, b=2),
+            )
+            return tile
+
+        def deal_scales(dst, raw):
+            nc.vector.tensor_copy(
+                dst.rearrange("p (t m) -> p t m", t=PACK),
+                raw[:].rearrange("p (m t) -> p t m", t=PACK),
+            )
+
+        def place_rows(planes):
+            words = planes[:].bitcast(I32)
+            for r in range(1, 4):
+                nc.sync.dma_start(words[r:P:32, :], words[8 * r : P : 32, :])
+
+        def bank(index, shape, name):
+            return psum.tile(shape, F32, name=name, tag="bank%d" % index)
+
+        offs_l = load_list("offs_l", offs)
+        w1s = load_scales(nc.sync, "w1s", w1_scales, H, "w1s")
+        xs = load_scales(nc.sync, "xs", x_scales, T, "xs")
+        w1w = load_fp4(nc.sync, "w1w", w1_words, "w1w")
+        xw = keep.tile([P, T], I32, name="xw", align_bytes=64)
+        nc.sync.dma_start(xw[:], x_words[0].rearrange("p n t -> p (n t)").bitcast(I32))
+        n1_l = load_list("n1_l", n1)
+        n2_l = load_list("n2_l", n2)
+        two_l = load_list("two_l", two)
+        n3_l = load_list("n3_l", n3)
+        n4_l = load_list("n4_l", n4)
+        half_c = keep.tile([P, 1], F32, name="half_c")
+        nc.vector.memset(half_c[:], 0.5)
+
+        planes1 = keep.tile([P, S + H], U8, name="planes1", align_bytes=64)
+        deal_scales(planes1[:, S:], w1s)
+        xs_offs = keep.tile([P, S], U8, name="xs_offs", tag="xs_offs", align_bytes=64)
+        nc.vector.tensor_copy(xs_offs[:], xs[:].indirect(offs_l[:]))
+        nc.vector.tensor_copy(planes1[:, :S].bitcast(I32), xs_offs[:].bitcast(I32))
+        place_rows(planes1)
+        gain = keep.tile([P, PACK], F32, name="gain", tag="xs_offs", align_bytes=64)
+        nc.sync.dma_start(gain[:], gn.rearrange("(p t) o -> p (t o)", t=PACK))
+        w1d = deal_words("w1d", w1w)
+
+        w23s = keep.tile([P, 2 * N], U8, name="w23s", tag="w1w", align_bytes=64)
+        for i, src in enumerate((w2_scales, w3_scales)):
+            rows = src[0].bitcast(I32).unsqueeze(1).to_broadcast([16, 8, N // 4])
+            nc.sync.dma_start(w23s[:, i * N : (i + 1) * N].bitcast(I32), rows)
+        v = [keep.tile([P, S], F32, name="v%d" % t) for t in range(PACK)]
+        y = {}
+        for h in range(2):
+            cols = slice(h * HALF, (h + 1) * HALF)
+            xg = keep.tile([P, HALF], U32, name="xw_offs%d" % h, tag="xw_offs%d" % h, align_bytes=64)
+            nc.vector.tensor_copy(xg[:], xw[:].bitcast(U32).indirect(entries(offs_l, h * HALF, HALF)))
+            for t in range(PACK):
+                y[t, h] = bank(PACK * h + t, [P, HALF], "y%d%d" % (t, h))
+                nc.tensor.matmul_mx(
+                    out=y[t, h][:], lhsT=w1d[:, 256 * t : 256 * (t + 1)].bitcast(FP4X4),
+                    lhsT_scale=planes1[:, S + P * t : S + P * (t + 1)],
+                    rhs=xg[:].bitcast(FP8X4), rhs_scale=planes1[:, cols], start=True, stop=True,
+                )
+        w3w = load_fp4(nc.sync, "w3w", w3_words, "xw_offs0")
+        w2w = load_fp4(nc.sync, "w2w", w2_words, "xw_offs1")
+        xw_two = keep.tile([P, S], U32, name="xw_two", align_bytes=64)
+        nc.vector.tensor_copy(xw_two[:], xw[:].bitcast(U32).indirect(two_l[:]))
+        for t in range(PACK):
+            for h in range(2):
+                cols = slice(h * HALF, (h + 1) * HALF)
+                if t == 0 or (t == 1 and h == 0):
+                    nc.scalar.activation(v[t][:, cols], y[t, h][:], ACT.Copy, scale=gain[:, t : t + 1])
+                else:
+                    nc.vector.tensor_scalar(v[t][:, cols], y[t, h][:], gain[:, t : t + 1], None, ALU.mult)
+
+        xs_two = keep.tile([P, S], U8, name="xs_two", tag="w1d", align_bytes=64)
+        nc.vector.tensor_copy(xs_two[:], xs[:].indirect(two_l[:]))
+        planes2 = keep.tile([P, S + 2 * N], U8, name="planes2", align_bytes=64)
+        nc.vector.tensor_copy(planes2[:, :S].bitcast(I32), xs_two[:].bitcast(I32))
+        nc.vector.tensor_copy(
+            planes2[:, S:].rearrange("p (w t m) -> p w t m", w=2, t=PACK),
+            w23s[:].rearrange("p (w m t) -> p w t m", w=2, t=PACK),
+        )
+        place_rows(planes2)
+        w3d = deal_words("w3d", w3w)
+        w2d = deal_words("w2d", w2w)
+
+        part = keep.tile([P, PACK, S], F32, name="part")
+        for t in range(PACK):
+            a = keep.tile([P, S], F32, name="a%d" % t)
+            for h in range(2):
+                nc.scalar.activation(
+                    a[:, h * HALF : (h + 1) * HALF], v[t][:].indirect(entries(n1_l, h * HALF, HALF)), ACT.Copy, scale=0.75
+                )
+            nc.vector.tensor_tensor(part[:, t, :], a[:], v[t][:], ALU.subtract)
+
+        hs = keep.tile([P, PACK, S], F32, name="hs")
+        groups = ((0, 1), (2, 3)), ((0, 1, 2, 3),), ((0,), (1,), (2,), (3,))
+        next_bank = 0
+        for index, (first, count) in enumerate(PIECES):
+            cols = slice(first, first + count)
+            b = keep.tile([P, PACK, count], F32, name="b%d" % index)
+            for t in range(PACK):
+                nc.scalar.activation(b[:, t, :], v[t][:].indirect(entries(n2_l, first, count)), ACT.Copy, scale=0.75)
+            zb = keep.tile([P, PACK * count], BF16, name="zb%d" % index, align_bytes=64)
+            nc.vector.tensor_tensor(
+                zb[:].rearrange("p (c i t) -> p c t i", i=4, t=PACK),
+                part[:, :, cols].rearrange("p t (c i) -> p c t i", i=4),
+                b[:].rearrange("p t (c i) -> p c t i", i=4),
+                ALU.add,
+            )
+            zw = keep.tile([P, count], U32, name="zw%d" % index, align_bytes=64)
+            zs = keep.tile([P, count], U8, name="zs%d" % index, align_bytes=64)
+            nc.vector.quantize_mx(zw[:].bitcast(FP8X4), zs[:], zb[:])
+            for members in groups[index]:
+                acc = bank(next_bank, [P, len(members), count], "h%d" % next_bank)
+                next_bank = next_bank + 1
+                for i, t in enumerate(members):
+                    nc.tensor.matmul_mx(
+                        out=acc[:, i, :], lhsT=w3d[:, 256 * t : 256 * (t + 1)].bitcast(FP4X4),
+                        lhsT_scale=planes2[:, S + N + P * t : S + N + P * (t + 1)],
+                        rhs=xw_two[:, cols].bitcast(FP8X4), rhs_scale=planes2[:, cols], start=(i == 0), stop=False,
+                    )
+                for i, t in enumerate(members):
+                    nc.tensor.matmul_mx(
+                        out=acc[:, i, :], lhsT=w2d[:, 256 * t : 256 * (t + 1)].bitcast(FP4X4),
+                        lhsT_scale=planes2[:, S + P * t : S + P * (t + 1)],
+                        rhs=zw[:].bitcast(FP8X4), rhs_scale=zs[:], start=False, stop=(i == len(members) - 1),
+                    )
+                dst = hs[:, members[0] : members[-1] + 1, cols]
+                if index < len(PIECES) - 1 or members[0] == 0:
+                    nc.scalar.copy(dst, acc[:])
+                else:
+                    nc.vector.tensor_copy(dst, acc[:])
+
+        st = keep.tile([P, PACK, S], F32, name="st")
+        inv = keep.tile([P, PACK, S], F32, name="inv")
+        for t in range(PACK):
+            g = keep.tile([P, S], F32, name="g%d" % t)
+            for h in range(2):
+                nc.scalar.activation(
+                    g[:, h * HALF : (h + 1) * HALF], hs[:, t, :].indirect(entries(n3_l, h * HALF, HALF)), ACT.Copy
+                )
+            nc.vector.tensor_tensor(st[:, t, :], hs[:, t, :], g[:], ALU.subtract)
+            size = keep.tile([P, S], F32, name="size%d" % t)
+            nc.vector.scalar_tensor_tensor(size[:], st[:, t, :], -1.0, st[:, t, :], ALU.mult, ALU.max)
+            root = keep.tile([P, S], F32, name="root%d" % t)
+            nc.scalar.activation(root[:], size[:], ACT.Abs_reciprocal_sqrt, bias=half_c[:])
+            nc.vector.tensor_tensor(inv[:, t, :], root[:], root[:], ALU.mult)
+
+        out_rows = out_0.rearrange("(p t) j -> p t j", t=PACK)
+        out_words = out_1[0].rearrange("p n t -> p (n t)").bitcast(I32)
+        ow = keep.tile([P, S], U32, name="ow", align_bytes=64)
+        osc = keep.tile([P, S], U8, name="osc", align_bytes=64)
+        for index, (first, count) in enumerate(OUT_PIECES):
+            cols = slice(first, first + count)
+            f = keep.tile([P, PACK, count], F32, name="f%d" % index)
+            for t in range(PACK):
+                nc.scalar.activation(f[:, t, :], inv[:, t, :].indirect(entries(n4_l, first, count)), ACT.Copy)
+            o = keep.tile([P, PACK, count], F32, name="o%d" % index)
+            for t in range(0, PACK, 2):
+                nc.vector.tensor_tensor(o[:, t : t + 2, :], st[:, t : t + 2, cols], f[:, t : t + 2, :], ALU.mult)
+            nc.sync.dma_start(out_rows[:, :, cols], o[:])
+            ob = keep.tile([P, PACK * count], BF16, name="ob%d" % index, align_bytes=64)
+            nc.vector.tensor_copy(
+                ob[:].rearrange("p (c i t) -> p c t i", i=4, t=PACK),
+                o[:].rearrange("p t (c i) -> p c t i", i=4),
+            )
+            nc.vector.quantize_mx(ow[:, cols].bitcast(FP8X4), osc[:, cols], ob[:])
+            nc.sync.dma_start(out_words[:, cols], ow[:, cols].bitcast(I32))
+        out_scales = out_2[0].bitcast(I32)
+        for q in range(4):
+            queue = nc.sync if q % 2 else nc.scalar
+            queue.dma_start(out_scales[4 * q : 4 * q + 4, :], osc[32 * q : 32 * q + 4, :].bitcast(I32))

@@ -18,7 +18,7 @@ K, T, S, N, H = 512, 2048, 512, 512, 512
 PACK = 4
 HALF = S // 2
 PIECES = ((0, 256), (256, 128), (384, 128))
-OUT_PIECES = ((0, 128), (128, 128), (256, 128), (384, 128))
+OUT_PIECES = ((0, 256), (256, 128), (384, 128))
 FLOPS = 3 * 2 * K * H * S
 
 
@@ -52,8 +52,8 @@ def tile_picked_hmixlaphopn_none_po_kernel(
             queue.dma_start(tile[:].bitcast(I32), src[0].bitcast(I32))
             return tile
 
-        def deal_words(name, raw):
-            tile = keep.tile([P, 2 * H], U8, name=name, tag=name, align_bytes=64)
+        def deal_words(name, raw, tag):
+            tile = keep.tile([P, 2 * H], U8, name=name, tag=tag, align_bytes=64)
             nc.vector.tensor_copy(
                 tile[:].rearrange("p (t m b) -> p t m b", t=PACK, b=2),
                 raw[:].rearrange("p (m t b) -> p t m b", t=PACK, b=2),
@@ -66,10 +66,10 @@ def tile_picked_hmixlaphopn_none_po_kernel(
                 raw[:].rearrange("p (m t) -> p t m", t=PACK),
             )
 
-        def place_rows(planes):
+        def place_rows(queue, planes):
             words = planes[:].bitcast(I32)
             for r in range(1, 4):
-                nc.sync.dma_start(words[r:P:32, :], words[8 * r : P : 32, :])
+                queue.dma_start(words[r:P:32, :], words[8 * r : P : 32, :])
 
         def bank(index, shape, name):
             return psum.tile(shape, F32, name=name, tag="bank%d" % index)
@@ -77,57 +77,60 @@ def tile_picked_hmixlaphopn_none_po_kernel(
         offs_l = load_list("offs_l", offs)
         w1s = load_scales(nc.sync, "w1s", w1_scales, H, "w1s")
         xs = load_scales(nc.sync, "xs", x_scales, T, "xs")
+        two_l = load_list("two_l", two)
         w1w = load_fp4(nc.sync, "w1w", w1_words, "w1w")
         xw = keep.tile([P, T], I32, name="xw", align_bytes=64)
         nc.sync.dma_start(xw[:], x_words[0].rearrange("p n t -> p (n t)").bitcast(I32))
         n1_l = load_list("n1_l", n1)
         n2_l = load_list("n2_l", n2)
-        two_l = load_list("two_l", two)
         n3_l = load_list("n3_l", n3)
         n4_l = load_list("n4_l", n4)
         half_c = keep.tile([P, 1], F32, name="half_c")
         nc.vector.memset(half_c[:], 0.5)
+        warm = keep.tile([P, 1], F32, name="warm")
+        nc.scalar.activation(warm[:], half_c[:], ACT.Abs_reciprocal_sqrt, bias=half_c[:])
 
         planes1 = keep.tile([P, S + H], U8, name="planes1", align_bytes=64)
         deal_scales(planes1[:, S:], w1s)
         xs_offs = keep.tile([P, S], U8, name="xs_offs", tag="xs_offs", align_bytes=64)
         nc.vector.tensor_copy(xs_offs[:], xs[:].indirect(offs_l[:]))
         nc.vector.tensor_copy(planes1[:, :S].bitcast(I32), xs_offs[:].bitcast(I32))
-        place_rows(planes1)
+        place_rows(nc.scalar, planes1)
         gain = keep.tile([P, PACK], F32, name="gain", tag="xs_offs", align_bytes=64)
-        nc.sync.dma_start(gain[:], gn.rearrange("(p t) o -> p (t o)", t=PACK))
-        w1d = deal_words("w1d", w1w)
+        nc.scalar.dma_start(gain[:], gn.rearrange("(p t) o -> p (t o)", t=PACK))
+        w1d = deal_words("w1d", w1w, "w1d")
 
-        w23s = keep.tile([P, 2 * N], U8, name="w23s", tag="w1w", align_bytes=64)
+        w23s = keep.tile([P, 2 * N], U8, name="w23s", align_bytes=64)
         for i, src in enumerate((w2_scales, w3_scales)):
             rows = src[0].bitcast(I32).unsqueeze(1).to_broadcast([16, 8, N // 4])
             nc.sync.dma_start(w23s[:, i * N : (i + 1) * N].bitcast(I32), rows)
         v = [keep.tile([P, S], F32, name="v%d" % t) for t in range(PACK)]
         y = {}
+        xg = []
         for h in range(2):
-            cols = slice(h * HALF, (h + 1) * HALF)
-            xg = keep.tile([P, HALF], U32, name="xw_offs%d" % h, tag="xw_offs%d" % h, align_bytes=64)
-            nc.vector.tensor_copy(xg[:], xw[:].bitcast(U32).indirect(entries(offs_l, h * HALF, HALF)))
-            for t in range(PACK):
-                y[t, h] = bank(PACK * h + t, [P, HALF], "y%d%d" % (t, h))
+            xg.append(keep.tile([P, HALF], U32, name="xw_offs%d" % h, tag="xw_offs%d" % h, align_bytes=64))
+            nc.vector.tensor_copy(xg[h][:], xw[:].bitcast(U32).indirect(entries(offs_l, h * HALF, HALF)))
+        for t in range(PACK):
+            for h in range(2):
+                y[t, h] = bank(2 * t + h, [P, HALF], "y%d%d" % (t, h))
                 nc.tensor.matmul_mx(
                     out=y[t, h][:], lhsT=w1d[:, 256 * t : 256 * (t + 1)].bitcast(FP4X4),
                     lhsT_scale=planes1[:, S + P * t : S + P * (t + 1)],
-                    rhs=xg[:].bitcast(FP8X4), rhs_scale=planes1[:, cols], start=True, stop=True,
+                    rhs=xg[h][:].bitcast(FP8X4), rhs_scale=planes1[:, h * HALF : (h + 1) * HALF], start=True, stop=True,
                 )
-        w3w = load_fp4(nc.sync, "w3w", w3_words, "xw_offs0")
-        w2w = load_fp4(nc.sync, "w2w", w2_words, "xw_offs1")
+        w3w = load_fp4(nc.sync, "w3w", w3_words, "w3w")
+        w2w = load_fp4(nc.sync, "w2w", w2_words, "w2w")
         xw_two = keep.tile([P, S], U32, name="xw_two", align_bytes=64)
         nc.vector.tensor_copy(xw_two[:], xw[:].bitcast(U32).indirect(two_l[:]))
         for t in range(PACK):
             for h in range(2):
                 cols = slice(h * HALF, (h + 1) * HALF)
-                if t == 0 or (t == 1 and h == 0):
+                if t == 0:
                     nc.scalar.activation(v[t][:, cols], y[t, h][:], ACT.Copy, scale=gain[:, t : t + 1])
                 else:
                     nc.vector.tensor_scalar(v[t][:, cols], y[t, h][:], gain[:, t : t + 1], None, ALU.mult)
 
-        xs_two = keep.tile([P, S], U8, name="xs_two", tag="w1d", align_bytes=64)
+        xs_two = keep.tile([P, S], U8, name="xs_two", align_bytes=64)
         nc.vector.tensor_copy(xs_two[:], xs[:].indirect(two_l[:]))
         planes2 = keep.tile([P, S + 2 * N], U8, name="planes2", align_bytes=64)
         nc.vector.tensor_copy(planes2[:, :S].bitcast(I32), xs_two[:].bitcast(I32))
@@ -135,9 +138,9 @@ def tile_picked_hmixlaphopn_none_po_kernel(
             planes2[:, S:].rearrange("p (w t m) -> p w t m", w=2, t=PACK),
             w23s[:].rearrange("p (w m t) -> p w t m", w=2, t=PACK),
         )
-        place_rows(planes2)
-        w3d = deal_words("w3d", w3w)
-        w2d = deal_words("w2d", w2w)
+        place_rows(nc.sync, planes2)
+        w3d = deal_words("w3d", w3w, "xw_offs1")
+        w2d = deal_words("w2d", w2w, "w1d")
 
         part = keep.tile([P, PACK, S], F32, name="part")
         for t in range(PACK):
@@ -148,19 +151,23 @@ def tile_picked_hmixlaphopn_none_po_kernel(
                 )
             nc.vector.tensor_tensor(part[:, t, :], a[:], v[t][:], ALU.subtract)
 
-        hs = keep.tile([P, PACK, S], F32, name="hs")
-        groups = ((0, 1), (2, 3)), ((0, 1, 2, 3),), ((0,), (1,), (2,), (3,))
+        hs = keep.tile([P, PACK + 1, S], F32, name="hs")
+        nc.gpsimd.memset(hs[:, PACK, :], 0.0)
+        groups = ((2, 3), (0, 1)), ((0, 1, 2, 3),), ((3,), (2,), (1,), (0,))
+        late = keep.tile([P, PACK, HALF], F32, name="late", tag="xs_offs", align_bytes=64)
+        early = keep.tile([P, PACK, HALF], F32, name="early")
         next_bank = 0
+        deferred = []
         for index, (first, count) in enumerate(PIECES):
             cols = slice(first, first + count)
-            b = keep.tile([P, PACK, count], F32, name="b%d" % index)
+            b = early[:] if first < HALF else late[:, :, first - HALF : first - HALF + count]
             for t in range(PACK):
                 nc.scalar.activation(b[:, t, :], v[t][:].indirect(entries(n2_l, first, count)), ACT.Copy, scale=0.75)
             zb = keep.tile([P, PACK * count], BF16, name="zb%d" % index, align_bytes=64)
             nc.vector.tensor_tensor(
                 zb[:].rearrange("p (c i t) -> p c t i", i=4, t=PACK),
                 part[:, :, cols].rearrange("p t (c i) -> p c t i", i=4),
-                b[:].rearrange("p t (c i) -> p c t i", i=4),
+                b.rearrange("p t (c i) -> p c t i", i=4),
                 ALU.add,
             )
             zw = keep.tile([P, count], U32, name="zw%d" % index, align_bytes=64)
@@ -182,38 +189,47 @@ def tile_picked_hmixlaphopn_none_po_kernel(
                         rhs=zw[:].bitcast(FP8X4), rhs_scale=zs[:], start=False, stop=(i == len(members) - 1),
                     )
                 dst = hs[:, members[0] : members[-1] + 1, cols]
-                if index < len(PIECES) - 1 or members[0] == 0:
+                if PACK - 1 in members or len(members) > 1:
                     nc.scalar.copy(dst, acc[:])
                 else:
-                    nc.vector.tensor_copy(dst, acc[:])
+                    deferred.append((-members[0], index, dst, acc))
+        for order, index, dst, acc in sorted(deferred, key=lambda d: d[:2]):
+            nc.vector.tensor_copy(dst, acc[:])
 
         st = keep.tile([P, PACK, S], F32, name="st")
         inv = keep.tile([P, PACK, S], F32, name="inv")
-        for t in range(PACK):
+        roots = {}
+
+        def square(t):
+            nc.vector.tensor_tensor(inv[:, t, :], roots[t][:], roots[t][:], ALU.mult)
+
+        for t in reversed(range(PACK)):
             g = keep.tile([P, S], F32, name="g%d" % t)
-            for h in range(2):
-                nc.scalar.activation(
-                    g[:, h * HALF : (h + 1) * HALF], hs[:, t, :].indirect(entries(n3_l, h * HALF, HALF)), ACT.Copy
-                )
+            window = hs[:, t : t + 2, :].rearrange("p a j -> p (a j)")
+            nc.scalar.activation(g[:], window.indirect(n3_l[:]), ACT.Copy)
             nc.vector.tensor_tensor(st[:, t, :], hs[:, t, :], g[:], ALU.subtract)
-            size = keep.tile([P, S], F32, name="size%d" % t)
+            if t == 0:
+                square(PACK - 1)
+            size = keep.tile([P, S], F32, name="size%d" % t, tag="size%d" % t)
             nc.vector.scalar_tensor_tensor(size[:], st[:, t, :], -1.0, st[:, t, :], ALU.mult, ALU.max)
-            root = keep.tile([P, S], F32, name="root%d" % t)
-            nc.scalar.activation(root[:], size[:], ACT.Abs_reciprocal_sqrt, bias=half_c[:])
-            nc.vector.tensor_tensor(inv[:, t, :], root[:], root[:], ALU.mult)
+            roots[t] = keep.tile([P, S], F32, name="root%d" % t, tag="root%d" % t)
+            nc.scalar.activation(roots[t][:], size[:], ACT.Abs_reciprocal_sqrt, bias=half_c[:])
+        for t in reversed(range(PACK - 1)):
+            square(t)
 
         out_rows = out_0.rearrange("(p t) j -> p t j", t=PACK)
         out_words = out_1[0].rearrange("p n t -> p (n t)").bitcast(I32)
         ow = keep.tile([P, S], U32, name="ow", align_bytes=64)
         osc = keep.tile([P, S], U8, name="osc", align_bytes=64)
+        f_early = keep.tile([P, PACK, HALF], F32, name="f_early")
+        f_late = keep.tile([P, PACK, HALF], F32, name="f_late", tag="root0")
         for index, (first, count) in enumerate(OUT_PIECES):
             cols = slice(first, first + count)
-            f = keep.tile([P, PACK, count], F32, name="f%d" % index)
-            for t in range(PACK):
-                nc.scalar.activation(f[:, t, :], inv[:, t, :].indirect(entries(n4_l, first, count)), ACT.Copy)
+            f = f_early[:] if first < HALF else f_late[:, :, first - HALF : first - HALF + count]
             o = keep.tile([P, PACK, count], F32, name="o%d" % index)
-            for t in range(0, PACK, 2):
-                nc.vector.tensor_tensor(o[:, t : t + 2, :], st[:, t : t + 2, cols], f[:, t : t + 2, :], ALU.mult)
+            for t in reversed(range(PACK)):
+                nc.scalar.activation(f[:, t, :], inv[:, t, :].indirect(entries(n4_l, first, count)), ACT.Copy)
+                nc.vector.tensor_tensor(o[:, t, :], st[:, t, cols], f[:, t, :], ALU.mult)
             nc.sync.dma_start(out_rows[:, :, cols], o[:])
             ob = keep.tile([P, PACK * count], BF16, name="ob%d" % index, align_bytes=64)
             nc.vector.tensor_copy(

@@ -77,10 +77,10 @@ def tile_picked_hmixlaphopn_none_po_kernel(
         offs_l = load_list("offs_l", offs)
         w1s = load_scales(nc.sync, "w1s", w1_scales, H, "w1s")
         xs = load_scales(nc.sync, "xs", x_scales, T, "xs")
-        two_l = load_list("two_l", two)
         w1w = load_fp4(nc.sync, "w1w", w1_words, "w1w")
         xw = keep.tile([P, T], I32, name="xw", align_bytes=64)
         nc.sync.dma_start(xw[:], x_words[0].rearrange("p n t -> p (n t)").bitcast(I32))
+        two_l = load_list("two_l", two)
         n1_l = load_list("n1_l", n1)
         n2_l = load_list("n2_l", n2)
         n3_l = load_list("n3_l", n3)
@@ -105,33 +105,33 @@ def tile_picked_hmixlaphopn_none_po_kernel(
             rows = src[0].bitcast(I32).unsqueeze(1).to_broadcast([16, 8, N // 4])
             nc.sync.dma_start(w23s[:, i * N : (i + 1) * N].bitcast(I32), rows)
         v = [keep.tile([P, S], F32, name="v%d" % t) for t in range(PACK)]
-        y = {}
-        xg = []
-        for h in range(2):
-            xg.append(keep.tile([P, HALF], U32, name="xw_offs%d" % h, tag="xw_offs%d" % h, align_bytes=64))
-            nc.vector.tensor_copy(xg[h][:], xw[:].bitcast(U32).indirect(entries(offs_l, h * HALF, HALF)))
-        for t in range(PACK):
-            for h in range(2):
-                y[t, h] = bank(2 * t + h, [P, HALF], "y%d%d" % (t, h))
-                nc.tensor.matmul_mx(
-                    out=y[t, h][:], lhsT=w1d[:, 256 * t : 256 * (t + 1)].bitcast(FP4X4),
-                    lhsT_scale=planes1[:, S + P * t : S + P * (t + 1)],
-                    rhs=xg[h][:].bitcast(FP8X4), rhs_scale=planes1[:, h * HALF : (h + 1) * HALF], start=True, stop=True,
-                )
+        xg = keep.tile([P, S], U32, name="xw_offs", tag="xw_offs", align_bytes=64)
+        for first in (0, HALF):
+            nc.vector.tensor_copy(xg[:, first : first + HALF], xw[:].bitcast(U32).indirect(entries(offs_l, first, HALF)))
+        spans = [(0, 0, HALF), (0, HALF, HALF)] + [(t, 0, S) for t in range(1, PACK)]
+        y = []
+        for index, (t, first, count) in enumerate(spans):
+            y.append(bank(index, [P, count], "y%d" % index))
+            nc.tensor.matmul_mx(
+                out=y[index][:], lhsT=w1d[:, 256 * t : 256 * (t + 1)].bitcast(FP4X4),
+                lhsT_scale=planes1[:, S + P * t : S + P * (t + 1)],
+                rhs=xg[:, first : first + count].bitcast(FP8X4), rhs_scale=planes1[:, first : first + count],
+                start=True, stop=True,
+            )
         w3w = load_fp4(nc.sync, "w3w", w3_words, "w3w")
         w2w = load_fp4(nc.sync, "w2w", w2_words, "w2w")
         xw_two = keep.tile([P, S], U32, name="xw_two", align_bytes=64)
         nc.vector.tensor_copy(xw_two[:], xw[:].bitcast(U32).indirect(two_l[:]))
-        for t in range(PACK):
-            for h in range(2):
-                cols = slice(h * HALF, (h + 1) * HALF)
-                if t == 0:
-                    nc.scalar.activation(v[t][:, cols], y[t, h][:], ACT.Copy, scale=gain[:, t : t + 1])
-                else:
-                    nc.vector.tensor_scalar(v[t][:, cols], y[t, h][:], gain[:, t : t + 1], None, ALU.mult)
+        for index, (t, first, count) in enumerate(spans):
+            dst = v[t][:, first : first + count]
+            if t == 0:
+                nc.scalar.activation(dst, y[index][:], ACT.Copy, scale=gain[:, t : t + 1])
+            else:
+                nc.vector.tensor_scalar(dst, y[index][:], gain[:, t : t + 1], None, ALU.mult)
+            if t == 1:
+                xs_two = keep.tile([P, S], U8, name="xs_two", align_bytes=64)
+                nc.vector.tensor_copy(xs_two[:], xs[:].indirect(two_l[:]))
 
-        xs_two = keep.tile([P, S], U8, name="xs_two", align_bytes=64)
-        nc.vector.tensor_copy(xs_two[:], xs[:].indirect(two_l[:]))
         planes2 = keep.tile([P, S + 2 * N], U8, name="planes2", align_bytes=64)
         nc.vector.tensor_copy(planes2[:, :S].bitcast(I32), xs_two[:].bitcast(I32))
         nc.vector.tensor_copy(
@@ -139,17 +139,18 @@ def tile_picked_hmixlaphopn_none_po_kernel(
             w23s[:].rearrange("p (w m t) -> p w t m", w=2, t=PACK),
         )
         place_rows(nc.sync, planes2)
-        w3d = deal_words("w3d", w3w, "xw_offs1")
         w2d = deal_words("w2d", w2w, "w1d")
 
-        part = keep.tile([P, PACK, S], F32, name="part")
+        part = keep.tile([P, PACK, S], F32, name="part", tag="w2w", align_bytes=64)
         for t in range(PACK):
-            a = keep.tile([P, S], F32, name="a%d" % t)
+            a = keep.tile([P, S], F32, name="a%d" % t, tag="a%d" % t, align_bytes=64)
             for h in range(2):
                 nc.scalar.activation(
                     a[:, h * HALF : (h + 1) * HALF], v[t][:].indirect(entries(n1_l, h * HALF, HALF)), ACT.Copy, scale=0.75
                 )
             nc.vector.tensor_tensor(part[:, t, :], a[:], v[t][:], ALU.subtract)
+            if t == PACK - 2:
+                w3d = deal_words("w3d", w3w, "a%d" % t)
 
         hs = keep.tile([P, PACK + 1, S], F32, name="hs")
         nc.gpsimd.memset(hs[:, PACK, :], 0.0)
@@ -165,9 +166,9 @@ def tile_picked_hmixlaphopn_none_po_kernel(
                 nc.scalar.activation(b[:, t, :], v[t][:].indirect(entries(n2_l, first, count)), ACT.Copy, scale=0.75)
             zb = keep.tile([P, PACK * count], BF16, name="zb%d" % index, align_bytes=64)
             nc.vector.tensor_tensor(
-                zb[:].rearrange("p (c i t) -> p c t i", i=4, t=PACK),
-                part[:, :, cols].rearrange("p t (c i) -> p c t i", i=4),
-                b.rearrange("p t (c i) -> p c t i", i=4),
+                zb[:].rearrange("p (c i t) -> p c t i", i=2, t=PACK),
+                part[:, :, cols].rearrange("p t (c i) -> p c t i", i=2),
+                b.rearrange("p t (c i) -> p c t i", i=2),
                 ALU.add,
             )
             zw = keep.tile([P, count], U32, name="zw%d" % index, align_bytes=64)
@@ -233,8 +234,8 @@ def tile_picked_hmixlaphopn_none_po_kernel(
             nc.sync.dma_start(out_rows[:, :, cols], o[:])
             ob = keep.tile([P, PACK * count], BF16, name="ob%d" % index, align_bytes=64)
             nc.vector.tensor_copy(
-                ob[:].rearrange("p (c i t) -> p c t i", i=4, t=PACK),
-                o[:].rearrange("p t (c i) -> p c t i", i=4),
+                ob[:].rearrange("p (c i t) -> p c t i", i=2, t=PACK),
+                o[:].rearrange("p t (c i) -> p c t i", i=2),
             )
             nc.vector.quantize_mx(ow[:, cols].bitcast(FP8X4), osc[:, cols], ob[:])
             nc.sync.dma_start(out_words[:, cols], ow[:, cols].bitcast(I32))

from contextlib import ExitStack

import concourse.mybir as mybir

F32 = mybir.dt.float32
BF16 = mybir.dt.bfloat16
I32 = mybir.dt.int32
U32 = mybir.dt.uint32
U16 = mybir.dt.uint16
U8 = mybir.dt.uint8
FP8X4 = mybir.dt.float8_e4m3fn_x4
FP4X4 = mybir.dt.float4_e2m1fn_x4
ALU = mybir.AluOpType
ACT = mybir.ActivationFunctionType

P = 128
K, T, S, N, H = 512, 2048, 512, 512, 512
PACK = 4
HALF = S // 2
PIECES = ((0, 256), (256, 128), (384, 128))
OUT_PIECES = ((0, 256), (256, 128), (384, 128))
FLOPS = 3 * 2 * K * H * S


def tile_picked_hmixlaphopn_none_po_kernel(
    tc, x_words, x_scales, w1_words, w1_scales, gn, w2_words, w2_scales, w3_words, w3_scales,
    offs, n1, n2, two, n3, n4, out_0, out_1, out_2,
):
    nc = tc.nc

    with ExitStack() as ctx:
        lists = ctx.enter_context(tc.tile_pool(name="lists", bufs=1))
        keep = ctx.enter_context(tc.tile_pool(name="keep", bufs=1))
        psum = ctx.enter_context(tc.psum_pool(name="psum", bufs=1))

        def load_list(name, src):
            tile = lists.tile([P, S // 16], U16, name=name)
            nc.sync.dma_start(tile[:], src)
            return tile

        def entries(tile, first, count):
            return tile[:, first // 16 : (first + count) // 16]

        def load_scales(queue, name, src, width, tag):
            tile = keep.tile([P, width], U8, name=name, tag=tag, align_bytes=64)
            rows = src[0].bitcast(I32).unsqueeze(1).to_broadcast([16, 8, width // 4])
            queue.dma_start(tile[:].bitcast(I32), rows)
            return tile

        def load_fp4(queue, name, src, tag):
            tile = keep.tile([P, 2 * H], U8, name=name, tag=tag, align_bytes=64)
            queue.dma_start(tile[:].bitcast(I32), src[0].bitcast(I32))
            return tile

        def deal_words(name, raw, tag):
            tile = keep.tile([P, 2 * H], U8, name=name, tag=tag, align_bytes=64)
            nc.vector.tensor_copy(
                tile[:].rearrange("p (t m b) -> p t m b", t=PACK, b=2),
                raw[:].rearrange("p (m t b) -> p t m b", t=PACK, b=2),
            )
            return tile

        def deal_scales(dst, raw):
            nc.vector.tensor_copy(
                dst.rearrange("p (t m) -> p t m", t=PACK),
                raw[:].rearrange("p (m t) -> p t m", t=PACK),
            )

        def place_rows(queue, planes):
            words = planes[:].bitcast(I32)
            for r in range(1, 4):
                queue.dma_start(words[r:P:32, :], words[8 * r : P : 32, :])

        def bank(index, shape, name):
            return psum.tile(shape, F32, name=name, tag="bank%d" % index)

        offs_l = load_list("offs_l", offs)
        w1s = load_scales(nc.sync, "w1s", w1_scales, H, "w1s")
        xs = load_scales(nc.sync, "xs", x_scales, T, "xs")
        w1w = load_fp4(nc.sync, "w1w", w1_words, "w1w")
        xw = keep.tile([P, T], I32, name="xw", align_bytes=64)
        nc.sync.dma_start(xw[:], x_words[0].rearrange("p n t -> p (n t)").bitcast(I32))
        two_l = load_list("two_l", two)
        n1_l = load_list("n1_l", n1)
        n2_l = load_list("n2_l", n2)
        n3_l = load_list("n3_l", n3)
        n4_l = load_list("n4_l", n4)
        half_c = keep.tile([P, 1], F32, name="half_c")
        nc.vector.memset(half_c[:], 0.5)
        warm = keep.tile([P, 1], F32, name="warm")
        nc.scalar.activation(warm[:], half_c[:], ACT.Abs_reciprocal_sqrt, bias=half_c[:])

        planes1 = keep.tile([P, S + H], U8, name="planes1", align_bytes=64)
        deal_scales(planes1[:, S:], w1s)
        xs_offs = keep.tile([P, S], U8, name="xs_offs", tag="xs_offs", align_bytes=64)
        nc.vector.tensor_copy(xs_offs[:], xs[:].indirect(offs_l[:]))
        nc.vector.tensor_copy(planes1[:, :S].bitcast(I32), xs_offs[:].bitcast(I32))
        place_rows(nc.scalar, planes1)
        gain = keep.tile([P, PACK], F32, name="gain", tag="xs_offs", align_bytes=64)
        nc.scalar.dma_start(gain[:], gn.rearrange("(p t) o -> p (t o)", t=PACK))
        w1d = deal_words("w1d", w1w, "w1d")

        w23s = keep.tile([P, 2 * N], U8, name="w23s", align_bytes=64)
        for i, src in enumerate((w2_scales, w3_scales)):
            rows = src[0].bitcast(I32).unsqueeze(1).to_broadcast([16, 8, N // 4])
            nc.sync.dma_start(w23s[:, i * N : (i + 1) * N].bitcast(I32), rows)
        v = [keep.tile([P, S], F32, name="v%d" % t) for t in range(PACK)]
        xg = keep.tile([P, S], U32, name="xw_offs", tag="xw_offs", align_bytes=64)
        for first in (0, HALF):
            nc.vector.tensor_copy(xg[:, first : first + HALF], xw[:].bitcast(U32).indirect(entries(offs_l, first, HALF)))
        spans = [(0, 0, HALF), (0, HALF, HALF)] + [(t, 0, S) for t in range(1, PACK)]
        y = []
        for index, (t, first, count) in enumerate(spans):
            y.append(bank(index, [P, count], "y%d" % index))
            nc.tensor.matmul_mx(
                out=y[index][:], lhsT=w1d[:, 256 * t : 256 * (t + 1)].bitcast(FP4X4),
                lhsT_scale=planes1[:, S + P * t : S + P * (t + 1)],
                rhs=xg[:, first : first + count].bitcast(FP8X4), rhs_scale=planes1[:, first : first + count],
                start=True, stop=True,
            )
        w3w = load_fp4(nc.sync, "w3w", w3_words, "w3w")
        w2w = load_fp4(nc.sync, "w2w", w2_words, "w2w")
        xw_two = keep.tile([P, S], U32, name="xw_two", align_bytes=64)
        nc.vector.tensor_copy(xw_two[:], xw[:].bitcast(U32).indirect(two_l[:]))
        for index, (t, first, count) in enumerate(spans):
            dst = v[t][:, first : first + count]
            if t == 0:
                nc.scalar.activation(dst, y[index][:], ACT.Copy, scale=gain[:, t : t + 1])
            else:
                nc.vector.tensor_scalar(dst, y[index][:], gain[:, t : t + 1], None, ALU.mult)
            if t == 1:
                xs_two = keep.tile([P, S], U8, name="xs_two", align_bytes=64)
                nc.vector.tensor_copy(xs_two[:], xs[:].indirect(two_l[:]))

        planes2 = keep.tile([P, S + 2 * N], U8, name="planes2", align_bytes=64)
        nc.vector.tensor_copy(planes2[:, :S].bitcast(I32), xs_two[:].bitcast(I32))
        nc.vector.tensor_copy(
            planes2[:, S:].rearrange("p (w t m) -> p w t m", w=2, t=PACK),
            w23s[:].rearrange("p (w m t) -> p w t m", w=2, t=PACK),
        )
        place_rows(nc.sync, planes2)
        w2d = deal_words("w2d", w2w, "w1d")

        part = keep.tile([P, PACK, S], F32, name="part", tag="w2w", align_bytes=64)
        for t in range(PACK):
            a = keep.tile([P, S], F32, name="a%d" % t, tag="a%d" % t, align_bytes=64)
            for h in range(2):
                nc.scalar.activation(
                    a[:, h * HALF : (h + 1) * HALF], v[t][:].indirect(entries(n1_l, h * HALF, HALF)), ACT.Copy, scale=0.75
                )
            nc.vector.tensor_tensor(part[:, t, :], a[:], v[t][:], ALU.subtract)
            if t == PACK - 2:
                w3d = deal_words("w3d", w3w, "a%d" % t)

        hs = keep.tile([P, PACK + 1, S], F32, name="hs")
        nc.gpsimd.memset(hs[:, PACK, :], 0.0)
        groups = ((2, 3), (0, 1)), ((0, 1, 2, 3),), ((3,), (2,), (1,), (0,))
        late = keep.tile([P, PACK, HALF], F32, name="late", tag="xs_offs", align_bytes=64)
        early = keep.tile([P, PACK, HALF], F32, name="early")
        next_bank = 0
        deferred = []
        for index, (first, count) in enumerate(PIECES):
            cols = slice(first, first + count)
            b = early[:] if first < HALF else late[:, :, first - HALF : first - HALF + count]
            for t in range(PACK):
                nc.scalar.activation(b[:, t, :], v[t][:].indirect(entries(n2_l, first, count)), ACT.Copy, scale=0.75)
            zb = keep.tile([P, PACK * count], BF16, name="zb%d" % index, align_bytes=64)
            nc.vector.tensor_tensor(
                zb[:].rearrange("p (c i t) -> p c t i", i=2, t=PACK),
                part[:, :, cols].rearrange("p t (c i) -> p c t i", i=2),
                b.rearrange("p t (c i) -> p c t i", i=2),
                ALU.add,
            )
            zw = keep.tile([P, count], U32, name="zw%d" % index, align_bytes=64)
            zs = keep.tile([P, count], U8, name="zs%d" % index, align_bytes=64)
            nc.vector.quantize_mx(zw[:].bitcast(FP8X4), zs[:], zb[:])
            for members in groups[index]:
                acc = bank(next_bank, [P, len(members), count], "h%d" % next_bank)
                next_bank = next_bank + 1
                for i, t in enumerate(members):
                    nc.tensor.matmul_mx(
                        out=acc[:, i, :], lhsT=w3d[:, 256 * t : 256 * (t + 1)].bitcast(FP4X4),
                        lhsT_scale=planes2[:, S + N + P * t : S + N + P * (t + 1)],
                        rhs=xw_two[:, cols].bitcast(FP8X4), rhs_scale=planes2[:, cols], start=(i == 0), stop=False,
                    )
                for i, t in enumerate(members):
                    nc.tensor.matmul_mx(
                        out=acc[:, i, :], lhsT=w2d[:, 256 * t : 256 * (t + 1)].bitcast(FP4X4),
                        lhsT_scale=planes2[:, S + P * t : S + P * (t + 1)],
                        rhs=zw[:].bitcast(FP8X4), rhs_scale=zs[:], start=False, stop=(i == len(members) - 1),
                    )
                dst = hs[:, members[0] : members[-1] + 1, cols]
                if PACK - 1 in members or len(members) > 1:
                    nc.scalar.copy(dst, acc[:])
                else:
                    deferred.append((-members[0], index, dst, acc))
        for order, index, dst, acc in sorted(deferred, key=lambda d: d[:2]):
            nc.vector.tensor_copy(dst, acc[:])

        st = keep.tile([P, PACK, S], F32, name="st")
        inv = keep.tile([P, PACK, S], F32, name="inv")
        roots = {}

        def square(t):
            nc.vector.tensor_tensor(inv[:, t, :], roots[t][:], roots[t][:], ALU.mult)

        for t in reversed(range(PACK)):
            g = keep.tile([P, S], F32, name="g%d" % t)
            window = hs[:, t : t + 2, :].rearrange("p a j -> p (a j)")
            nc.scalar.activation(g[:], window.indirect(n3_l[:]), ACT.Copy)
            nc.vector.tensor_tensor(st[:, t, :], hs[:, t, :], g[:], ALU.subtract)
            if t == 0:
                square(PACK - 1)
            size = keep.tile([P, S], F32, name="size%d" % t, tag="size%d" % t)
            nc.vector.scalar_tensor_tensor(size[:], st[:, t, :], -1.0, st[:, t, :], ALU.mult, ALU.max)
            roots[t] = keep.tile([P, S], F32, name="root%d" % t, tag="root%d" % t)
            nc.scalar.activation(roots[t][:], size[:], ACT.Abs_reciprocal_sqrt, bias=half_c[:])
        for t in reversed(range(PACK - 1)):
            square(t)

        out_rows = out_0.rearrange("(p t) j -> p t j", t=PACK)
        out_words = out_1[0].rearrange("p n t -> p (n t)").bitcast(I32)
        ow = keep.tile([P, S], U32, name="ow", align_bytes=64)
        osc = keep.tile([P, S], U8, name="osc", align_bytes=64)
        f_early = keep.tile([P, PACK, HALF], F32, name="f_early")
        f_late = keep.tile([P, PACK, HALF], F32, name="f_late", tag="root0")
        for index, (first, count) in enumerate(OUT_PIECES):
            cols = slice(first, first + count)
            f = f_early[:] if first < HALF else f_late[:, :, first - HALF : first - HALF + count]
            o = keep.tile([P, PACK, count], F32, name="o%d" % index)
            for t in reversed(range(PACK)):
                nc.scalar.activation(f[:, t, :], inv[:, t, :].indirect(entries(n4_l, first, count)), ACT.Copy)
                nc.vector.tensor_tensor(o[:, t, :], st[:, t, cols], f[:, t, :], ALU.mult)
            nc.sync.dma_start(out_rows[:, :, cols], o[:])
            ob = keep.tile([P, PACK * count], BF16, name="ob%d" % index, align_bytes=64)
            nc.vector.tensor_copy(
                ob[:].rearrange("p (c i t) -> p c t i", i=2, t=PACK),
                o[:].rearrange("p t (c i) -> p c t i", i=2),
            )
            nc.vector.quantize_mx(ow[:, cols].bitcast(FP8X4), osc[:, cols], ob[:])
            nc.sync.dma_start(out_words[:, cols], ow[:, cols].bitcast(I32))
        out_scales = out_2[0].bitcast(I32)
        for q in range(4):
            queue = nc.sync if q % 2 else nc.scalar
            queue.dma_start(out_scales[4 * q : 4 * q + 4, :], osc[32 * q : 32 * q + 4, :].bitcast(I32))
